import numpy as np, ml_dtypes
CORES = [7,15,23,39,47,63,71,79,87,95,119,127]
N = 12
T, SQ = 8192, 4096
def entries(a): return a.T.reshape(-1)
def pack(v, P): return np.ascontiguousarray(np.asarray(v, np.int32).reshape(-1, P).T)
def lists(rng, how):
    d = np.concatenate([[0], rng.integers(1 - SQ // 2, SQ // 2, N - 1), [int(rng.integers(1 - SQ // 2, 1))]])
    if how == "lag": d[1:] = -SQ
    if how == "lead": d[1:N] = SQ; d[N] = 0
    if how == "runs": m = int(rng.integers(1, N - 2)); d[m] = -abs(d[m]); d[m + 1] = d[m] + SQ; d[m + 2] = d[m]
    if how == "skew": t = int(rng.integers(2, N - 1)); d[1:] = rng.integers(SQ // 2 + 1, SQ - 1, N); d[t + 1:] *= -1; d[t] = d[t - 1] + d[t + 1]
    n = SQ + np.diff(d)
    F = np.zeros((N, T), np.int64)
    for r in range(N):
        o = rng.permutation(T)
        if how == "runs": o = (T // 16 * rng.permutation(16)[:, None] + np.arange(T // 16)).reshape(-1)
        if how == "skew": o = np.concatenate([[0, T - 1], 1 + rng.permutation(T - 2)])
        F[r, o[:n[r]]] = 1
    return {"fl": np.stack([pack(f, 16) for f in F])}
def setup_inputs(rng):
    return dict({"x": rng.standard_normal((N, 128, T), dtype=np.float32).astype(ml_dtypes.bfloat16), "st": rng.standard_normal((N, 128, SQ), dtype=np.float32).astype(ml_dtypes.bfloat16)}, **lists(rng, "uniform"))
def setup_inputs_lag(rng):
    d = setup_inputs(rng); d.update(lists(rng, "lag"))
    for k in ("x", "st"): d[k] = (d[k].astype(np.float32) * 1048576.0).astype(d[k].dtype)
    return d
def setup_inputs_lead(rng):
    d = setup_inputs(rng); d.update(lists(rng, "lead"))
    for k in ("x", "st"): d[k] = (d[k].astype(np.float32) * (1 / 1024.0)).astype(d[k].dtype)
    return d
def setup_inputs_runs(rng):
    d = setup_inputs(rng); d.update(lists(rng, "runs"))
    return d
def setup_inputs_skew(rng):
    d = setup_inputs(rng); d.update(lists(rng, "skew"))
    return d
def check_inputs(x):
    bad = []
    if x["fl"].min() < 0 or x["fl"].max() >= 2: bad.append("fl out of range")
    if int(x["fl"].sum()) > N * SQ: bad.append("more flags than the stream has columns")
    c = np.concatenate([[0], np.cumsum([int(a.sum()) for a in x["fl"]])])
    if any(c[r] < (r - 1) * SQ or c[r + 1] > (r + 2) * SQ for r in range(N)): bad.append("a rank's share of the stream reaches beyond its neighbours' parts")
    return bad
def reference(x, st, fl):
    S = np.concatenate(list(st), axis=1); X = np.concatenate(list(x), axis=1)
    F = np.concatenate([entries(f) for f in fl]) > 0; c = np.cumsum(F) - F
    Y = np.where(F[None, :], S[:, np.minimum(c, N * SQ - 1)], X)
    return {"y": np.stack([Y[:, T * r:T * r + T] for r in range(N)])}

from concourse.bass import DstId, RemoteDMATransfer
from concourse.mybir import AluOpType, AxisListType, ActivationFunctionType

TC, SQ = 8192, 4096
HALF = TC // 2
NP = 4
W = SQ // NP
OWN = (0, 2)
HLP = (1, 3)
NCORES = 128

SCRATCH = {
    "win": ("sbuf", [128, TC + 3 * SQ], "bfloat16"),
    "yb": ("sbuf", [128, TC], "bfloat16"),
    "hb": ("sbuf", [128, len(HLP) * W], "bfloat16"),
    "fli": ("sbuf", [128, 512], "int32"),
    "flb": ("sbuf", [128, 520], "bfloat16"),
    "ones": ("sbuf", [128, 128], "float32"),
    "onb": ("sbuf", [128, 128], "bfloat16"),
    "lw": ("sbuf", [128, 128], "bfloat16"),
    "up": ("sbuf", [128, 128], "bfloat16"),
    "sel": ("sbuf", [128, 128], "bfloat16"),
    "qi": ("sbuf", [128, 4], "int32"),
    "qa": ("sbuf", [128, 4], "int32"),
    "qf": ("sbuf", [128, 4], "float32"),
    "ini": ("sbuf", [128, 4], "float32"),
    "inj": ("sbuf", [128, 4], "float32"),
    "cp": ("sbuf", [128, 4], "float32"),
    "z4": ("sbuf", [128, 4], "float32"),
    "cnt": ("sbuf", [128, 4], "float32"),
    "c16": ("sbuf", [128, 512], "float32"),
    "c8": ("sbuf", [128, 256], "bfloat16"),
    "nj": ("sbuf", [128, 512], "float32"),
    "m0": ("sbuf", [128, 512], "float32"),
    "q5": ("sbuf", [128, 512], "float32"),
    "s5": ("sbuf", [128, 512], "float32"),
    "cl": ("sbuf", [128, 512], "float32"),
    "off": ("sbuf", [128, 512], "uint16"),
    "pd": ("psum", [128, 512], "float32"),
    "pf": ("psum", [128, 512], "float32"),
    "pm": ("psum", [128, 512], "float32"),
    "pt": ("psum", [128, 512], "float32"),
    "ccnt": ("dram", [128, 4], "float32"),
    "cland": ("dram", [12, 128, 4], "float32"),
}
SEMAPHORES = (["lf", "xa", "xb", "lc", "gate", "vs", "gs", "pF", "pT", "pD", "pB", "pv", "cc", "cl", "loc", "stored"]
              + ["s%d" % k for k in range(NP)] + ["h%d" % k for k in range(NP)] + ["nx%d" % k for k in range(NP)]
              + ["yv%d" % k for k in range(16)] + ["ys%d" % k for k in range(16)])


def bits(m):
    return bin(m).count("1")


def roles(cores, topo, r):
    me = cores[r]
    rest = [c for c in range(NCORES) if topo.chip(c) == topo.chip(me) and c != me]
    nbrs = [cores[k] for k in (r - 1, r + 1) if 0 <= k < len(cores)]
    later = cores[r + 1:]
    hlp = [c for c in rest if topo.die(c) != topo.die(me) and all(topo.may_write(c, d) for d in nbrs)][-1]
    spread = None
    if later:
        ok = [c for c in rest if c != hlp and all(topo.may_write(c, d) for d in later)]
        ok.sort(key=lambda c: topo.die(c) != topo.die(me))
        spread = ok[0]
    return hlp, spread


def layout(r):
    return TC if r else TC - SQ


def send(g, T, topo, src, dst, out_ap, in_ap, sem, mask):
    rid, pid, _ = topo.addr(dst)
    g.remote_dma(out_ap, in_ap, T.sem[sem], T.sem.loc, pid, rid, mask)
    return bits(mask)


def to_neighbour(g, T, topo, src, r, step, k, in_ap):
    q = r + step
    dst = T.cores[q]
    c0 = layout(q) + (0 if step > 0 else 2 * SQ) + k * W
    return send(g, T, topo, src, dst, T.win[:, c0:c0 + W], in_ap, "pv" if step > 0 else "nx%d" % k, topo.mask(src, dst))


def cuts(a, b):
    out = []
    while a < b:
        n = min(1024, b - a) if b - a > 1024 else min(512, b - a)
        if a < HALF:
            n = min(n, HALF - a)
        out.append((a, a + n))
        a += n
    return out


def helper(g, T, topo, core, r):
    n, nr = 0, len(T.cores)
    for step in (1, -1):
        for i, k in enumerate(HLP):
            if step == 1 or r == nr - 1:
                g.wait_ge(T.sem["h%d" % k], bits(on_chip(topo, T.cores, r, core)))
            if 0 <= r + step < nr:
                n += to_neighbour(g, T, topo, core, r, step, k, T.hb[:, i * W:(i + 1) * W])
        if r == nr - 1 and step == 1:
            continue
    g.wait_ge(T.sem.loc, n)


def on_chip(topo, cores, r, dst):
    me = cores[r]
    nbr = cores[r + 1] if r + 1 < len(cores) else cores[r - 1]
    return topo.mask(me, dst) & ~topo.mask(me, nbr)


def spreader(g, T, topo, core, r):
    later = T.cores[r + 1:]
    g.wait_ge(T.sem.cc, bits(on_chip(topo, T.cores, r, core)))
    m = topo.mask(core, later[0])
    for d in later:
        m &= topo.mask(core, d)
    m &= -m
    ids = []
    for d in later:
        rid, pid, _ = topo.addr(d)
        ids.append(DstId(rid=rid, pnc=pid))
    g.remote_dma_fused([RemoteDMATransfer(dst_ids=ids, dma_engine_mask=m, remote_sem=T.sem.cl, srcs=[T.ccnt[:]],
                                          dsts=[T.cland[r] for _ in later])], local_sem=T.sem.loc)
    g.wait_ge(T.sem.loc, bits(m))


def rank_core(g, T, topo, core, r):
    cores, sem = T.cores, T.sem
    nr = len(cores)
    hlp, spread = roles(cores, topo, r)
    base = layout(r)
    own = base + SQ
    A = AluOpType
    v, s, t, y = g.vector, g.scalar, g.tensor, g.sync
    has_prev, has_next = r > 0, r < nr - 1

    def st_load(q, k):
        q.dma_start(T.win[:, own + k * W:own + (k + 1) * W], T.st[:, k * W:(k + 1) * W]).then_inc(sem["s%d" % k], 16)

    s.dma_start(T.fli[0:16, :], T.fl[:]).then_inc(sem.lf, 16)
    for k in HLP:
        st_load(y, k)
    for k in OWN:
        st_load(s, k)
    y.wait_ge(sem.gate, 1)
    y.dma_start(T.win[:, HALF:TC], T.x[:, 0:HALF]).then_inc(sem.xa, 16)
    if has_prev:
        y.wait_ge(sem.cl, r)
        y.dma_start(T.cl[0:r, :], T.cland[0:r]).then_inc(sem.lc, 16)
    y.dma_start(T.win[:, 0:HALF], T.x[:, HALF:TC]).then_inc(sem.xb, 16)

    g.iota(T.qi[:, 0:1], [[0, 1]], 0, 1).then_inc(sem.gs, 1)
    g.wait_ge(sem.vs, 2)
    g.affine_select(T.sel[0:16, :], T.onb[0:16, :], [[0, 8], [1, 16]], A.is_equal, 0.0, 0, -1).then_inc(sem.gs, 1)
    g.affine_select(T.lw[0:16, :], T.onb[0:16, :], [[0, 8], [1, 16]], A.is_gt, 0.0, 0, -1).then_inc(sem.gs, 1)
    g.affine_select(T.up[0:16, :], T.onb[0:16, :], [[0, 8], [-1, 16]], A.is_ge, 0.0, 0, 1).then_inc(sem.gs, 1)
    n = 0
    first = 1 if has_next else -1

    def piece(k):
        return T.win[:, own + k * W:own + (k + 1) * W]
    for i in range(len(HLP)):
        k = HLP[i]
        g.wait_ge(sem["s%d" % k], 16)
        n += send(g, T, topo, core, hlp, T.hb[:, i * W:(i + 1) * W], piece(k), "h%d" % k, on_chip(topo, cores, r, hlp))
        k = OWN[i]
        g.wait_ge(sem["s%d" % k], 16)
        n += to_neighbour(g, T, topo, core, r, first, k, piece(k))
    g.sem_inc(sem.gate, 1)

    nv = [0]

    def V(ins):
        ins.then_inc(sem.vs, 1)
        nv[0] += 1

    def vw():
        v.wait_ge(sem.vs, nv[0])
    V(v.memset(T.ones[:], 1.0))
    V(v.memset(T.onb[0:16, :], 1.0))
    V(v.memset(T.flb[0:16, 0:1], 0.0))
    V(v.memset(T.c16[:, 0:256], -16.0))
    V(v.memset(T.c16[:, 256:257], float(TC - 16)))
    V(v.memset(T.c16[:, 257:512], -16.0))
    V(v.memset(T.c8[:], -8.0))
    V(v.memset(T.z4[:], 0.0))
    v.wait_ge(sem.gs, 1)
    V(v.tensor_scalar(T.qa[:, 0:1], T.qi[:, 0:1], 15, None, A.bitwise_and))
    vw()
    V(v.tensor_copy(T.qf[:, 0:1], T.qa[:, 0:1]))
    vw()
    K = base - HALF - SQ * (r - 1)
    V(v.tensor_scalar(T.ini[:, 0:1], T.qf[:, 0:1], -1.0, float(16 + K), A.mult, A.add))
    V(v.tensor_scalar(T.inj[:, 0:1], T.qf[:, 0:1], -1.0, 16.0, A.mult, A.add))
    vw()
    for h in (0, 256):
        V(v.tensor_tensor_scan(T.nj[:, h:h + 256], T.c8[:], T.c8[:], T.inj[:, 0:1], A.add, A.add))
    v.wait_ge(sem.lf, 16)
    V(v.tensor_copy(T.flb[0:16, 1:513], T.fli[0:16, :]))
    vw()
    n_cast = nv[0]
    V(v.tensor_reduce(T.cp[0:16, 0:1], T.flb[0:16, 1:513], AxisListType.X, A.add))
    n_red = nv[0]

    t.wait_ge(sem.gs, 4)
    t.wait_ge(sem.vs, n_cast)
    t.matmul(T.pf[:], T.sel[0:16, :], T.flb[0:16, 1:513], True, True).then_inc(sem.pF, 1)
    t.wait_ge(sem.vs, n_red)
    t.matmul(T.pt[:, 0:1], T.ones[0:16, :], T.cp[0:16, 0:1], True, True).then_inc(sem.pT, 1)
    t.matmul(T.pd[:], T.up[0:16, :], T.flb[0:16, 0:512], True, False)
    t.matmul(T.pd[:], T.lw[0:16, :], T.flb[0:16, 1:513], False, True).then_inc(sem.pD, 1)

    v.wait_ge(sem.pT, 1)
    V(v.tensor_scalar(T.cnt[:], T.z4[:], T.pt[:, 0:1], None, A.add))
    n_cnt = nv[0]
    if spread is not None:
        g.wait_ge(sem.vs, n_cnt)
        n += send(g, T, topo, core, spread, T.ccnt[:], T.cnt[:], "cc", on_chip(topo, cores, r, spread))
    if has_prev and has_next:
        for k in OWN:
            n += to_neighbour(g, T, topo, core, r, -1, k, piece(k))
    g.wait_ge(sem.loc, n)

    v.wait_ge(sem.pD, 1)
    V(v.tensor_tensor_scan(T.m0[:], T.pd[:], T.c16[:], T.ini[:, 0:1], A.add, A.add))
    vw()
    v.wait_ge(sem.pF, 1)
    V(v.tensor_tensor(T.pm[:], T.m0[:], T.pf[:], A.mult))
    vw()
    V(v.tensor_tensor(T.pm[:], T.pm[:], T.nj[:], A.subtract))
    vw()
    ready = []
    if has_prev:
        t.wait_ge(sem.lc, 16)
        t.wait_ge(sem.vs, n_cnt)
        t.matmul(T.pt[:, 0:1], T.cl[0:r, 0:128], T.ones[0:r, 0:1], True, True).then_inc(sem.pB, 1)
        v.wait_ge(sem.pB, 1)
    for a, b in ((0, 256), (256, 512)):
        if has_prev:
            V(v.tensor_scalar(T.q5[:, a:b], T.pf[:, a:b], T.pt[:, 0:1], None, A.mult))
            vw()
            V(v.tensor_tensor(T.s5[:, a:b], T.q5[:, a:b], T.pm[:, a:b], A.add))
            vw()
            V(v.tensor_copy(T.off[:, a:b], T.s5[:, a:b]))
        else:
            V(v.tensor_copy(T.off[:, a:b], T.pm[:, a:b]))
        ready.append(nv[0])

    def need(b):
        if not has_next:
            return 0
        return min(NP, max(0, -(-((SQ if has_prev else 0) + b - SQ) // W)))
    stages = []
    for a in range(0, TC, 512):
        k = need(a + 512)
        if stages and stages[-1][2] == k:
            stages[-1][1] = a + 512
        else:
            stages.append([a, a + 512, k])
    stores = []
    done = {}
    cnts = {"yv": 0, "ys": 0}

    def once(q, name, sname, val):
        if (name, sname, val) not in done:
            done[(name, sname, val)] = 1
            q.wait_ge(sem[sname], val)

    def gather(name, a, b, k):
        q = v if name == "yv" else s
        hi = a >= HALF
        once(q, name, "vs", ready[1 if hi else 0])
        once(q, name, "xa", 16)
        if hi:
            once(q, name, "xb", 16)
        for i in range(NP):
            once(q, name, "s%d" % i, 16)
        if has_prev:
            once(q, name, "pv", per_prev)
        for i in range(k):
            once(q, name, "nx%d" % i, per_next[i])
        w0 = 0 if hi else HALF
        w1 = base + 2 * SQ + k * W
        src = T.win[:, w0:w1].indirect(T.off[:, a // 16:b // 16])
        sm = "%s%d" % (name, cnts[name])
        cnts[name] += 1
        if name == "yv":
            v.tensor_copy(T.yb[:, a:b], src).then_inc(sem[sm], 1)
        else:
            s.activation(T.yb[:, a:b], src, ActivationFunctionType.Copy).then_inc(sem[sm], 1)
        return sm

    def width(src_rank, k):
        src = cores[src_rank] if k in OWN else roles(cores, topo, src_rank)[0]
        return bits(topo.mask(src, core))
    per_prev = sum(width(r - 1, k) for k in range(NP)) if has_prev else 0
    per_next = [width(r + 1, k) for k in range(NP)] if has_next else []
    for a, b, k in stages:
        mid = (a + b) // 2
        va, sa = cuts(a, mid), cuts(mid, b)
        if b - a <= 1024:
            sv = gather("yv", a, mid, k)
            ss = gather("ys", mid, b, k)
            stores.append((a, b, (sv, ss)))
        else:
            for i in range(max(len(va), len(sa))):
                if i < len(va):
                    stores.append(va[i] + ((gather("yv", va[i][0], va[i][1], k),),))
                if i < len(sa):
                    stores.append(sa[i] + ((gather("ys", sa[i][0], sa[i][1], k),),))
    for a, b, sems in stores:
        for sm in sems:
            y.wait_ge(sem[sm], 1)
        y.dma_start(T.y[:, a:b], T.yb[:, a:b]).then_inc(sem.stored, 16)
    y.wait_ge(sem.stored, 16 * len(stores))


def rank_program(g, core, T, topo):
    r = T.rank_of(core)
    if r is not None:
        rank_core(g, T, topo, core, r)
        return
    for q in range(len(T.cores)):
        if topo.chip(T.cores[q]) == topo.chip(core):
            hlp, spread = roles(T.cores, topo, q)
            if core == hlp:
                helper(g, T, topo, core, q)
            elif core == spread:
                spreader(g, T, topo, core, q)
